import numpy as np
import ml_dtypes


def mxq(x, axis, fmt="e4m3"):
    dtype, down = {"e4m3": (ml_dtypes.float8_e4m3fn, 7), "e5m2": (ml_dtypes.float8_e5m2, 14)}[fmt]
    v = np.moveaxis(np.asarray(x, np.float32).astype(ml_dtypes.bfloat16).astype(np.float64), axis, -1)
    blocks = v.reshape(v.shape[:-1] + (-1, 32))
    amax = np.abs(blocks).max(-1, keepdims=True)
    byte = np.maximum(np.where(amax > 0, np.frexp(amax)[1] - 1 + 127, 0) - down, 1)
    scale = np.exp2(byte - 127.0)
    codes = (blocks / scale).astype(np.float32).astype(dtype).astype(np.float64)
    return np.moveaxis((codes * scale).reshape(v.shape), -1, axis)


WIDE = False


def mx_kscale(k):
    if not WIDE:
        return np.ones(k)
    levels = np.array([10, -10, 5, -5, 0])
    if k % 512:
        return np.exp2(np.random.permutation(np.resize(levels, k // 32))).repeat(32)
    a = np.empty((k // 512, 16))
    for p in range(k // 512):
        a[p, :8] = np.random.permutation(np.resize(levels, 8))
        for g in range(8):
            far = levels[np.abs(levels - a[p, g]) >= 10]
            a[p, g + 8] = far[np.random.randint(len(far))]
    return np.exp2(a.ravel()).repeat(32)


def f64(x):
    return np.asarray(x).astype(np.float64)


def striped(idx):
    return np.tile(idx.reshape(-1, 16).T, (8, 1)).astype(np.uint16)


def unstriped(offs):
    return offs[:16].T.reshape(-1).astype(np.int64)


def pack_weight(w):
    k, n = w.shape
    w = f64(np.asarray(w, np.float32).astype(ml_dtypes.bfloat16)).reshape(k // 32, 32, n)
    amax = np.abs(w).max(1)
    byte = np.clip(np.where(amax > 0, np.frexp(amax)[1] - 1 + 127 - 7, 1), 1, 254)
    scaled = (w * np.exp2(127.0 - byte)[:, None, :]).reshape(k, n).astype(np.float32)
    words = np.ascontiguousarray(scaled.reshape(k // 512, 128, 4, n).transpose(0, 1, 3, 2)).astype(ml_dtypes.float8_e4m3fn).view(np.uint8)
    return words, np.ascontiguousarray(byte.astype(np.uint8).reshape(k // 512, 16, n))


def unpack_weight(words, scales):
    g, p, n, _ = words.shape
    vals = np.ascontiguousarray(words).view(ml_dtypes.float8_e4m3fn).astype(np.float64) * np.repeat(np.exp2(scales.astype(np.float64) - 127.0), 8, axis=1)[..., None]
    return vals.transpose(0, 1, 3, 2).reshape(g * 512, n)


def relu(v):
    return np.maximum(v, 0.0)


K, T, S, V, H, N = 512, 4096, 1536, 768, 512, 128


def setup_inputs():
    n = np.random.standard_normal
    s = mx_kscale(K)[:, None]
    u = mx_kscale(H)
    packed_xT = pack_weight(n((K, T)) * s)
    packed_w2 = pack_weight(n((H, N)) / np.sqrt(2 * H) / u[:, None])
    packed_w3 = pack_weight(n((H, N)) / np.sqrt(2 * H) / u[:, None])
    return {
        "x_words": packed_xT[0],
        "x_scales": packed_xT[1],
        "w1": (n((K, H)) / np.sqrt(K) / s * u).astype(np.float32),
        "w2_words": packed_w2[0],
        "w2_scales": packed_w2[1],
        "w3_words": packed_w3[0],
        "w3_scales": packed_w3[1],
        "offs": striped(np.random.permutation(T)[:S]),
    }


def reference(x_words, x_scales, w1, w2_words, w2_scales, w3_words, w3_scales, offs):
    xq = unpack_weight(x_words, x_scales)[:, unstriped(offs)]
    h = relu(mxq(f64(w1), 0, "e4m3").T @ xq)
    low = 0.5 * (h[:, :V] + h[:, V:2 * V])
    high = 0.5 * (h[:, :V] - h[:, V:2 * V])
    return unpack_weight(w2_words, w2_scales).T @ mxq(low, 0, "e4m3") + unpack_weight(w3_words, w3_scales).T @ mxq(high, 0, "e4m3")

@@ -1,0 +1,132 @@
+from contextlib import ExitStack
+
+import concourse.mybir as mybir
+
+K, T, S, V, H, N = 512, 4096, 1536, 768, 512, 128
+FLOPS = 2 * K * H * S + 2 * 2 * H * N * V
+
+F32 = mybir.dt.float32
+BF16 = mybir.dt.bfloat16
+I32 = mybir.dt.int32
+U32 = mybir.dt.uint32
+U16 = mybir.dt.uint16
+U8 = mybir.dt.uint8
+FP8X4 = mybir.dt.float8_e4m3fn_x4
+ALU = mybir.AluOpType
+ACT = mybir.ActivationFunctionType
+
+P = 128
+G = 128
+SLICE = 512
+
+
+def tile_picked_haar_relu_p_kernel(tc, x_words, x_scales, w1, w2_words, w2_scales, w3_words, w3_scales, offs, out):
+    nc = tc.nc
+    with ExitStack() as ctx:
+        keep = ctx.enter_context(tc.tile_pool(name="keep", bufs=1))
+        ring = ctx.enter_context(tc.tile_pool(name="ring", bufs=3))
+        psum = ctx.enter_context(tc.psum_pool(name="psum", bufs=3))
+        psum_out = ctx.enter_context(tc.psum_pool(name="psum_out", bufs=2))
+
+        offsets = keep.tile([P, S // 16], U16, name="offsets")
+        nc.sync.dma_start(offsets[:], offs)
+
+        x_table = keep.tile([P, T], U32, name="x_table", align_bytes=64)
+        nc.sync.dma_start(x_table[:].bitcast(I32), x_words[0].rearrange("p n r -> p (n r)").bitcast(I32))
+
+        scale_table = keep.tile([P, T], U8, name="scale_table", align_bytes=64)
+        nc.vector.memset(scale_table[:].bitcast(I32), 0)
+        nc.scalar.dma_start(scale_table[:].bitcast(I32)[0:P:8, :], x_scales[0].bitcast(I32))
+
+        w1_rows = w1.rearrange("(p j) c -> p j c", j=4)
+        w1_half = []
+        for u in range(2):
+            raw = keep.tile([P, 4, H // 2], F32, name="w1_raw%d" % u)
+            nc.sync.dma_start(raw[:], w1_rows[:, :, u * (H // 2):(u + 1) * (H // 2)])
+            w1_half.append(raw)
+
+        band_scales = keep.tile([P, 2 * N], U8, name="band_scales", align_bytes=64)
+        nc.vector.memset(band_scales[:].bitcast(I32), 0)
+        x_plane = keep.tile([P, S], U8, name="x_plane", align_bytes=64)
+        nc.vector.memset(x_plane[:].bitcast(I32), 0)
+        for b, scales in enumerate((w2_scales, w3_scales)):
+            for q in range(4):
+                nc.gpsimd.dma_start(
+                    band_scales[:].bitcast(I32)[32 * q:32 * q + 4, b * (N // 4):(b + 1) * (N // 4)],
+                    scales[0, 4 * q:4 * q + 4, :].bitcast(I32))
+
+        picked_scales = keep.tile([P, S], U8, name="picked_scales", align_bytes=64)
+        nc.vector.tensor_copy(picked_scales[:], scale_table[:].indirect(offsets[:]))
+        for r in range(4):
+            nc.sync.dma_start(x_plane[:].bitcast(I32)[r:P:32, :], picked_scales[:].bitcast(I32)[8 * r:P:32, :])
+
+        band_words = []
+        for b, words in enumerate((w2_words, w3_words)):
+            codes = keep.tile([P, N], U32, name="band_words%d" % b, align_bytes=64)
+            nc.sync.dma_start(codes[:].bitcast(I32), words[0].rearrange("p n r -> p (n r)").bitcast(I32))
+            band_words.append(codes)
+
+        picked = {}
+        for s in (2, 0, 1):
+            words = keep.tile([P, SLICE], U32, name="picked%d" % s, align_bytes=64)
+            cols = slice(s * (SLICE // 16), (s + 1) * (SLICE // 16))
+            nc.vector.tensor_copy(words[:], x_table[:].indirect(offsets[:, cols]))
+            picked[s] = words
+
+        w1_bf = keep.tile([P, 4 * H], BF16, name="w1_bf", align_bytes=64)
+        w1_dealt = w1_bf[:].rearrange("p (t m j) -> p m t j", t=4, j=4)
+        for u in range(2):
+            nc.scalar.activation(w1_dealt[:, 64 * u:64 * (u + 1), :, :],
+                                 w1_half[u][:].rearrange("p j (m t) -> p m t j", t=4), ACT.Copy)
+        w1_codes = keep.tile([P, H], U32, name="w1_codes", align_bytes=64)
+        w1_plane = keep.tile([P, H], U8, name="w1_plane", align_bytes=64)
+        for t in range(4):
+            nc.vector.quantize_mx(out=w1_codes[:, P * t:P * (t + 1)].bitcast(FP8X4),
+                                  scales=w1_plane[:, P * t:P * (t + 1)],
+                                  in_=w1_bf[:, 4 * P * t:4 * P * (t + 1)])
+
+        def first_product(entry, tag):
+            bank = psum.tile([P, 4, G], F32, name=tag)
+            words = picked[entry // SLICE][:, entry % SLICE:entry % SLICE + G]
+            for t in range(4):
+                nc.tensor.matmul_mx(out=bank[:, t, :], lhsT=w1_codes[:, P * t:P * (t + 1)].bitcast(FP8X4),
+                                    lhsT_scale=w1_plane[:, P * t:P * (t + 1)],
+                                    rhs=words.bitcast(FP8X4), rhs_scale=x_plane[:, entry:entry + G],
+                                    start=True, stop=True)
+            return bank[:].rearrange("p t v -> p v t")
+
+        def bands(g):
+            second = ring.tile([P, G, 4], F32, name="second")
+            nc.scalar.activation(second[:], first_product(V + G * g, "bank_second"), ACT.Relu)
+            first = first_product(G * g, "bank_first")
+            both = ring.tile([P, 2, G, 4], BF16, name="both", align_bytes=64)
+            for b, op in enumerate((ALU.add, ALU.subtract)):
+                nc.vector.scalar_tensor_tensor(both[:, b, :, :], first, 0.0, second[:], ALU.max, op)
+            return both
+
+        result = keep.tile([P, V], F32, name="result")
+
+        def second_product(g, both):
+            codes = ring.tile([P, 2 * G], U32, name="codes", align_bytes=64)
+            plane = ring.tile([P, 2 * G], U8, name="plane", align_bytes=64)
+            nc.vector.quantize_mx(out=codes[:].bitcast(FP8X4), scales=plane[:],
+                                  in_=both[:].rearrange("p b v t -> p (b v t)"))
+            acc = psum_out.tile([P, G], F32, name="acc")
+            for b in range(2):
+                nc.tensor.matmul_mx(out=acc[:], lhsT=band_words[b][:].bitcast(FP8X4),
+                                    lhsT_scale=band_scales[:, N * b:N * (b + 1)],
+                                    rhs=codes[:, G * b:G * (b + 1)].bitcast(FP8X4),
+                                    rhs_scale=plane[:, G * b:G * (b + 1)], start=(b == 0), stop=(b == 1))
+            nc.scalar.activation(result[:, G * g:G * (g + 1)], acc[:], ACT.Copy, scale=0.5)
+
+        order = (2, 3, 4, 5, 0, 1)
+        store_after = {3: (2, 4), 5: (4, 6), 0: (0, 1), 1: (1, 2)}
+        pending = None
+        for g in order + (None,):
+            made = None if g is None else (g, bands(g))
+            if pending is not None:
+                second_product(*pending)
+                if pending[0] in store_after:
+                    a, b = store_after[pending[0]]
+                    nc.sync.dma_start(out[:, G * a:G * b], result[:, G * a:G * b])
+            pending = made

@@ -1,6 +1,7 @@
 from contextlib import ExitStack
 
 import concourse.mybir as mybir
+from concourse.masks import make_identity
 
 K, T, S, V, H, N = 512, 4096, 1536, 768, 512, 128
 FLOPS = 2 * K * H * S + 2 * 2 * H * N * V
@@ -28,37 +29,24 @@ def tile_picked_haar_relu_p_kernel(tc, x_words, x_scales, w1, w2_words, w2_scale
         psum = ctx.enter_context(tc.psum_pool(name="psum", bufs=3))
         psum_out = ctx.enter_context(tc.psum_pool(name="psum_out", bufs=2))
 
+        scale_table = keep.tile([P, T], U8, name="scale_table", tag="scales", align_bytes=64)
+        nc.vector.memset(scale_table[:].bitcast(I32), 0)
+        w1_rows = w1.rearrange("(p j) c -> p j c", j=4)
+        w1_half = [keep.tile([P, 4, H // 2], F32, name="w1_raw%d" % u) for u in range(2)]
+
+        def load_w1(u, j, k):
+            nc.sync.dma_start(w1_half[u][:, j:k, :], w1_rows[:, j:k, u * (H // 2):(u + 1) * (H // 2)])
+
+        load_w1(0, 0, 4)
         offsets = keep.tile([P, S // 16], U16, name="offsets")
         nc.sync.dma_start(offsets[:], offs)
 
+        load_w1(1, 0, 1)
+        load_w1(1, 1, 2)
+        nc.sync.dma_start(scale_table[:].bitcast(I32)[0:P:8, :], x_scales[0].bitcast(I32))
+        load_w1(1, 2, 4)
         x_table = keep.tile([P, T], U32, name="x_table", align_bytes=64)
         nc.sync.dma_start(x_table[:].bitcast(I32), x_words[0].rearrange("p n r -> p (n r)").bitcast(I32))
-
-        scale_table = keep.tile([P, T], U8, name="scale_table", align_bytes=64)
-        nc.vector.memset(scale_table[:].bitcast(I32), 0)
-        nc.scalar.dma_start(scale_table[:].bitcast(I32)[0:P:8, :], x_scales[0].bitcast(I32))
-
-        w1_rows = w1.rearrange("(p j) c -> p j c", j=4)
-        w1_half = []
-        for u in range(2):
-            raw = keep.tile([P, 4, H // 2], F32, name="w1_raw%d" % u)
-            nc.sync.dma_start(raw[:], w1_rows[:, :, u * (H // 2):(u + 1) * (H // 2)])
-            w1_half.append(raw)
-
-        band_scales = keep.tile([P, 2 * N], U8, name="band_scales", align_bytes=64)
-        nc.vector.memset(band_scales[:].bitcast(I32), 0)
-        x_plane = keep.tile([P, S], U8, name="x_plane", align_bytes=64)
-        nc.vector.memset(x_plane[:].bitcast(I32), 0)
-        for b, scales in enumerate((w2_scales, w3_scales)):
-            for q in range(4):
-                nc.gpsimd.dma_start(
-                    band_scales[:].bitcast(I32)[32 * q:32 * q + 4, b * (N // 4):(b + 1) * (N // 4)],
-                    scales[0, 4 * q:4 * q + 4, :].bitcast(I32))
-
-        picked_scales = keep.tile([P, S], U8, name="picked_scales", align_bytes=64)
-        nc.vector.tensor_copy(picked_scales[:], scale_table[:].indirect(offsets[:]))
-        for r in range(4):
-            nc.sync.dma_start(x_plane[:].bitcast(I32)[r:P:32, :], picked_scales[:].bitcast(I32)[8 * r:P:32, :])
 
         band_words = []
         for b, words in enumerate((w2_words, w3_words)):
@@ -66,12 +54,20 @@ def tile_picked_haar_relu_p_kernel(tc, x_words, x_scales, w1, w2_words, w2_scale
             nc.sync.dma_start(codes[:].bitcast(I32), words[0].rearrange("p n r -> p (n r)").bitcast(I32))
             band_words.append(codes)
 
-        picked = {}
-        for s in (2, 0, 1):
-            words = keep.tile([P, SLICE], U32, name="picked%d" % s, align_bytes=64)
-            cols = slice(s * (SLICE // 16), (s + 1) * (SLICE // 16))
-            nc.vector.tensor_copy(words[:], x_table[:].indirect(offsets[:, cols]))
-            picked[s] = words
+        x_plane = keep.tile([P, S], U8, name="x_plane", align_bytes=64)
+        nc.vector.memset(x_plane[:].bitcast(I32), 0)
+        picked_scales = keep.tile([P, S], U8, name="picked_scales", align_bytes=64)
+        nc.vector.tensor_copy(picked_scales[:], scale_table[:].indirect(offsets[:]))
+        for r in range(4):
+            nc.sync.dma_start(x_plane[:].bitcast(I32)[r:P:32, :], picked_scales[:].bitcast(I32)[8 * r:P:32, :])
+
+        band_scales = keep.tile([P, 2 * N], U8, name="band_scales", tag="scales", align_bytes=64)
+        nc.vector.memset(band_scales[:].bitcast(I32), 0)
+        for b, scales in enumerate((w2_scales, w3_scales)):
+            for q in range(4):
+                nc.sync.dma_start(
+                    band_scales[:].bitcast(I32)[32 * q:32 * q + 4, b * (N // 4):(b + 1) * (N // 4)],
+                    scales[0, 4 * q:4 * q + 4, :].bitcast(I32))
 
         w1_bf = keep.tile([P, 4 * H], BF16, name="w1_bf", align_bytes=64)
         w1_dealt = w1_bf[:].rearrange("p (t m j) -> p m t j", t=4, j=4)
@@ -85,6 +81,13 @@ def tile_picked_haar_relu_p_kernel(tc, x_words, x_scales, w1, w2_words, w2_scale
                                   scales=w1_plane[:, P * t:P * (t + 1)],
                                   in_=w1_bf[:, 4 * P * t:4 * P * (t + 1)])
 
+        picked = {}
+        for s in (2, 0, 1):
+            words = keep.tile([P, SLICE], U32, name="picked%d" % s, align_bytes=64)
+            cols = slice(s * (SLICE // 16), (s + 1) * (SLICE // 16))
+            nc.vector.tensor_copy(words[:], x_table[:].indirect(offsets[:, cols]))
+            picked[s] = words
+
         def first_product(entry, tag):
             bank = psum.tile([P, 4, G], F32, name=tag)
             words = picked[entry // SLICE][:, entry % SLICE:entry % SLICE + G]
@@ -95,38 +98,100 @@ def tile_picked_haar_relu_p_kernel(tc, x_words, x_scales, w1, w2_words, w2_scale
                                     start=True, stop=True)
             return bank[:].rearrange("p t v -> p v t")
 
-        def bands(g):
-            second = ring.tile([P, G, 4], F32, name="second")
-            nc.scalar.activation(second[:], first_product(V + G * g, "bank_second"), ACT.Relu)
-            first = first_product(G * g, "bank_first")
-            both = ring.tile([P, 2, G, 4], BF16, name="both", align_bytes=64)
-            for b, op in enumerate((ALU.add, ALU.subtract)):
-                nc.vector.scalar_tensor_tensor(both[:, b, :, :], first, 0.0, second[:], ALU.max, op)
-            return both
-
         result = keep.tile([P, V], F32, name="result")
 
-        def second_product(g, both):
-            codes = ring.tile([P, 2 * G], U32, name="codes", align_bytes=64)
-            plane = ring.tile([P, 2 * G], U8, name="plane", align_bytes=64)
-            nc.vector.quantize_mx(out=codes[:].bitcast(FP8X4), scales=plane[:],
-                                  in_=both[:].rearrange("p b v t -> p (b v t)"))
-            acc = psum_out.tile([P, G], F32, name="acc")
-            for b in range(2):
+        def rectified(bank, name):
+            values = ring.tile([P, G, 4], F32, name=name, bufs=6)
+            nc.scalar.activation(values[:], bank, ACT.Relu)
+            return values
+
+        def band(values, op, first, second):
+            nc.vector.scalar_tensor_tensor(values, first, 0.0, second[:], ALU.max, op)
+
+        def quantised(values, name):
+            width = values.shape[1] // 4
+            codes = ring.tile([P, width], U32, name=name + "_codes", align_bytes=64)
+            plane = ring.tile([P, width], U8, name=name + "_plane", align_bytes=64)
+            nc.vector.quantize_mx(out=codes[:].bitcast(FP8X4), scales=plane[:], in_=values)
+            return codes, plane
+
+        def second_product(g, low, high, last=False):
+            acc = psum.tile([P, G], F32, name="bank_second") if last else psum_out.tile([P, G], F32, name="acc")
+            for b, (codes, plane) in enumerate((low, high)):
                 nc.tensor.matmul_mx(out=acc[:], lhsT=band_words[b][:].bitcast(FP8X4),
                                     lhsT_scale=band_scales[:, N * b:N * (b + 1)],
-                                    rhs=codes[:, G * b:G * (b + 1)].bitcast(FP8X4),
-                                    rhs_scale=plane[:, G * b:G * (b + 1)], start=(b == 0), stop=(b == 1))
+                                    rhs=codes.bitcast(FP8X4), rhs_scale=plane, start=(b == 0), stop=(b == 1))
             nc.scalar.activation(result[:, G * g:G * (g + 1)], acc[:], ACT.Copy, scale=0.5)
 
-        order = (2, 3, 4, 5, 0, 1)
-        store_after = {3: (2, 4), 5: (4, 6), 0: (0, 1), 1: (1, 2)}
-        pending = None
-        for g in order + (None,):
-            made = None if g is None else (g, bands(g))
-            if pending is not None:
-                second_product(*pending)
-                if pending[0] in store_after:
-                    a, b = store_after[pending[0]]
-                    nc.sync.dma_start(out[:, G * a:G * b], result[:, G * a:G * b])
-            pending = made
+        identity = keep.tile([P, P], F32, name="identity")
+        make_identity(nc, identity[:])
+
+        def turned_product(entry, name):
+            bank = psum.tile([P, H], F32, name="bank_second")
+            words = picked[entry // SLICE][:, entry % SLICE:entry % SLICE + G]
+            nc.tensor.matmul_mx(out=bank[:], lhsT=words.bitcast(FP8X4), lhsT_scale=x_plane[:, entry:entry + G],
+                                rhs=w1_codes[:].bitcast(FP8X4), rhs_scale=w1_plane[:], start=True, stop=True)
+            values = keep.tile([P, H], F32, name=name)
+            nc.scalar.activation(values[:], bank[:], ACT.Relu)
+            return values
+
+        def turned_sum(values, first, second):
+            bank = psum.tile([P, 4, G], F32, name="bank_second")
+            for t in range(4):
+                for k, part in enumerate((first, second)):
+                    nc.tensor.matmul(bank[:, t, :], part[:, P * t:P * (t + 1)], identity[:],
+                                     start=(k == 0), stop=(k == 1), is_transpose=True)
+            nc.scalar.copy(values, bank[:].rearrange("p t v -> p v t"))
+
+        def store(a, b):
+            nc.sync.dma_start(out[:, G * a:G * b], result[:, G * a:G * b])
+
+        def both_bands(g, both):
+            codes, plane = quantised(both[:].rearrange("p b v t -> p (b v t)"), "both")
+            return g, (codes[:, :G], plane[:, :G]), (codes[:, G:], plane[:, G:])
+
+        second = {3: rectified(first_product(V + G * 3, "bank_second"), "second")}
+        turned_second = turned_product(V + G * 2, "turned_second")
+        bank = {3: first_product(G * 3, "bank_first")}
+        second[4] = rectified(first_product(V + G * 4, "bank_second"), "second")
+        turned_first = turned_product(G * 2, "turned_first")
+        turned_negative = keep.tile([P, H], F32, name="turned_negative")
+        nc.gpsimd.tensor_scalar(turned_negative[:], turned_second[:], -1.0, 0.0, ALU.mult, ALU.add)
+        second[5] = rectified(first_product(V + G * 5, "bank_second"), "second")
+        extra = ring.tile([P, 2, G, 4], BF16, name="both", align_bytes=64)
+        band(extra[:, 0, :, :], ALU.add, bank[3], second[3])
+        band(extra[:, 1, :, :], ALU.subtract, bank[3], second[3])
+        extra_group = 3
+        for shared, alone in ((4, 5), (0, 1)):
+            if shared not in second:
+                second[shared] = rectified(first_product(V + G * shared, "bank_second"), "second")
+            bank[shared] = first_product(G * shared, "bank_first")
+            shared_first = rectified(bank[shared], "first")
+            if alone not in second:
+                second[alone] = rectified(first_product(V + G * alone, "bank_second"), "second")
+            bank[alone] = first_product(G * alone, "bank_first")
+            if shared == 0:
+                extra = ring.tile([P, 2, G, 4], BF16, name="both", align_bytes=64)
+                turned_sum(extra[:, 0, :, :], turned_first, turned_second)
+                turned_sum(extra[:, 1, :, :], turned_first, turned_negative)
+                extra_group = 2
+            shared_high = keep.tile([P, G, 4], BF16, name="shared_high", align_bytes=64)
+            alone_high = ring.tile([P, G, 4], BF16, name="alone_high", align_bytes=64)
+            lows = ring.tile([P, 2, G, 4], BF16, name="lows", align_bytes=64)
+            nc.gpsimd.tensor_tensor(shared_high[:], shared_first[:], second[shared][:], ALU.subtract)
+            band(alone_high[:], ALU.subtract, bank[alone], second[alone])
+            band(lows[:, 0, :, :], ALU.add, bank[alone], second[alone])
+            band(lows[:, 1, :, :], ALU.add, bank[shared], second[shared])
+            if shared != 0:
+                second_product(*both_bands(extra_group, extra))
+            alone_codes, alone_plane = quantised(alone_high[:].rearrange("p v t -> p (v t)"), "alone_high")
+            low_codes, low_plane = quantised(lows[:].rearrange("p g v t -> p (g v t)"), "lows")
+            shared_codes, shared_plane = quantised(shared_high[:].rearrange("p v t -> p (v t)"), "shared_high")
+            second_product(alone, (low_codes[:, :G], low_plane[:, :G]), (alone_codes[:], alone_plane[:]))
+            second_product(shared, (low_codes[:, G:], low_plane[:, G:]), (shared_codes[:], shared_plane[:]))
+            if shared == 0:
+                store(0, 2)
+                second_product(*both_bands(extra_group, extra), last=True)
+                store(2, 3)
+            else:
+                store(3, 6)

@@ -19,74 +19,89 @@ ACT = mybir.ActivationFunctionType
 P = 128
 G = 128
 SLICE = 512
+TABLE_ROW = P - 16
+HALF = H // 2
 
 
 def tile_picked_haar_relu_p_kernel(tc, x_words, x_scales, w1, w2_words, w2_scales, w3_words, w3_scales, offs, out):
     nc = tc.nc
     with ExitStack() as ctx:
         keep = ctx.enter_context(tc.tile_pool(name="keep", bufs=1))
+        reused = ctx.enter_context(tc.tile_pool(name="reused", bufs=1))
         ring = ctx.enter_context(tc.tile_pool(name="ring", bufs=3))
         psum = ctx.enter_context(tc.psum_pool(name="psum", bufs=3))
         psum_out = ctx.enter_context(tc.psum_pool(name="psum_out", bufs=2))
 
-        scale_table = keep.tile([P, T], U8, name="scale_table", tag="scales", align_bytes=64)
-        nc.vector.memset(scale_table[:].bitcast(I32), 0)
-        w1_rows = w1.rearrange("(p j) c -> p j c", j=4)
-        w1_half = [keep.tile([P, 4, H // 2], F32, name="w1_raw%d" % u) for u in range(2)]
-
-        def load_w1(u, j, k):
-            nc.sync.dma_start(w1_half[u][:, j:k, :], w1_rows[:, j:k, u * (H // 2):(u + 1) * (H // 2)])
-
-        load_w1(0, 0, 4)
-        offsets = keep.tile([P, S // 16], U16, name="offsets")
-        nc.sync.dma_start(offsets[:], offs)
-
-        load_w1(1, 0, 1)
-        load_w1(1, 1, 2)
-        nc.sync.dma_start(scale_table[:].bitcast(I32)[0:P:8, :], x_scales[0].bitcast(I32))
-        load_w1(1, 2, 4)
-        x_table = keep.tile([P, T], U32, name="x_table", align_bytes=64)
-        nc.sync.dma_start(x_table[:].bitcast(I32), x_words[0].rearrange("p n r -> p (n r)").bitcast(I32))
-
-        band_words = []
-        for b, words in enumerate((w2_words, w3_words)):
-            codes = keep.tile([P, N], U32, name="band_words%d" % b, align_bytes=64)
-            nc.sync.dma_start(codes[:].bitcast(I32), words[0].rearrange("p n r -> p (n r)").bitcast(I32))
-            band_words.append(codes)
-
+        scale_table = reused.tile([P, T], U8, name="scale_table", align_bytes=64, offset=0)
+        nc.gpsimd.memset(scale_table[:].bitcast(I32)[:TABLE_ROW, :], 0)
         x_plane = keep.tile([P, S], U8, name="x_plane", align_bytes=64)
         nc.vector.memset(x_plane[:].bitcast(I32), 0)
+        identity = keep.tile([P, P], F32, name="identity")
+        make_identity(nc, identity[:])
+
+        offsets = keep.tile([P, S // 16], U16, name="offsets")
+        nc.sync.dma_start(offsets[:], offs)
+        nc.sync.dma_start(scale_table[:].bitcast(I32)[TABLE_ROW:, :], x_scales[0].bitcast(I32))
+        w1_rows = w1.rearrange("(p j) c -> p j c", j=4)
+        w1_raw = [keep.tile([P, 4, HALF], F32, name="w1_raw%d" % u) for u in range(2)]
+        x_table = keep.tile([P, T], U32, name="x_table", align_bytes=64)
+        x_rows = x_words[0].rearrange("p n r -> p (n r)").bitcast(I32)
+
+        def load_band_words(words, tile):
+            nc.sync.dma_start(tile[:].bitcast(I32), words[0].rearrange("p n r -> p (n r)").bitcast(I32))
+            return tile
+
+        nc.sync.dma_start(x_table[:].bitcast(I32), x_rows)
+        for u in range(2):
+            nc.sync.dma_start(w1_raw[u][:], w1_rows[:, :, u * HALF:(u + 1) * HALF])
+
         picked_scales = keep.tile([P, S], U8, name="picked_scales", align_bytes=64)
         nc.vector.tensor_copy(picked_scales[:], scale_table[:].indirect(offsets[:]))
         for r in range(4):
-            nc.sync.dma_start(x_plane[:].bitcast(I32)[r:P:32, :], picked_scales[:].bitcast(I32)[8 * r:P:32, :])
+            nc.sync.dma_start(x_plane[:].bitcast(I32)[r:P:32, :], picked_scales[:].bitcast(I32)[TABLE_ROW + r:P:4, :])
 
-        band_scales = keep.tile([P, 2 * N], U8, name="band_scales", tag="scales", align_bytes=64)
-        nc.vector.memset(band_scales[:].bitcast(I32), 0)
+        band_words = [load_band_words(words, reused.tile([P, N], U32, name="band_words%d" % b, align_bytes=64, offset=4 * N * b))
+                      for b, words in enumerate((w2_words, w3_words))]
+        band_scales = reused.tile([P, 2 * N], U8, name="band_scales", align_bytes=64, offset=8 * N)
+        nc.gpsimd.memset(band_scales[:].bitcast(I32), 0)
         for b, scales in enumerate((w2_scales, w3_scales)):
             for q in range(4):
                 nc.sync.dma_start(
                     band_scales[:].bitcast(I32)[32 * q:32 * q + 4, b * (N // 4):(b + 1) * (N // 4)],
                     scales[0, 4 * q:4 * q + 4, :].bitcast(I32))
 
-        w1_bf = keep.tile([P, 4 * H], BF16, name="w1_bf", align_bytes=64)
-        w1_dealt = w1_bf[:].rearrange("p (t m j) -> p m t j", t=4, j=4)
-        for u in range(2):
-            nc.scalar.activation(w1_dealt[:, 64 * u:64 * (u + 1), :, :],
-                                 w1_half[u][:].rearrange("p j (m t) -> p m t j", t=4), ACT.Copy)
         w1_codes = keep.tile([P, H], U32, name="w1_codes", align_bytes=64)
         w1_plane = keep.tile([P, H], U8, name="w1_plane", align_bytes=64)
-        for t in range(4):
-            nc.vector.quantize_mx(out=w1_codes[:, P * t:P * (t + 1)].bitcast(FP8X4),
-                                  scales=w1_plane[:, P * t:P * (t + 1)],
-                                  in_=w1_bf[:, 4 * P * t:4 * P * (t + 1)])
-
+        M = HALF // 4
         picked = {}
-        for s in (2, 0, 1):
-            words = keep.tile([P, SLICE], U32, name="picked%d" % s, align_bytes=64)
+
+        def gather_words(s, offset):
+            words = reused.tile([P, SLICE], U32, name="picked%d" % s, align_bytes=64, offset=offset)
             cols = slice(s * (SLICE // 16), (s + 1) * (SLICE // 16))
             nc.vector.tensor_copy(words[:], x_table[:].indirect(offsets[:, cols]))
             picked[s] = words
+
+        def cast_half(u, cut):
+            values = reused.tile([P, 4, M, 4], BF16, name="w1_bf%d" % u, align_bytes=64, offset=T + 4 * H * u)
+            dealt = values[:].rearrange("p t m j -> p m j t")
+            source = w1_raw[u][:].rearrange("p j (m t) -> p m j t", t=4)
+            nc.scalar.activation(dealt[:, :cut], source[:, :cut], ACT.Copy)
+            if cut < M:
+                nc.vector.tensor_copy(dealt[:, cut:], source[:, cut:])
+            return values
+
+        def quantise_half(u, values):
+            for t in range(4):
+                cols = slice(P * t + M * u, P * t + M * (u + 1))
+                nc.vector.quantize_mx(out=w1_codes[:, cols].bitcast(FP8X4), scales=w1_plane[:, cols],
+                                      in_=values[:, t, :, :].rearrange("p m j -> p (m j)"))
+
+        gather_words(2, T + 8 * H)
+        gather_words(0, T + 12 * H)
+        halves = [cast_half(0, M), cast_half(1, M // 2)]
+        for u in range(2):
+            quantise_half(u, halves[u])
+        gather_words(1, T + 4 * H)
 
         def first_product(entry, tag):
             bank = psum.tile([P, 4, G], F32, name=tag)
@@ -98,35 +113,18 @@ def tile_picked_haar_relu_p_kernel(tc, x_words, x_scales, w1, w2_words, w2_scale
                                     start=True, stop=True)
             return bank[:].rearrange("p t v -> p v t")
 
-        result = keep.tile([P, V], F32, name="result")
-
         def rectified(bank, name):
             values = ring.tile([P, G, 4], F32, name=name, bufs=6)
             nc.scalar.activation(values[:], bank, ACT.Relu)
             return values
 
-        def band(values, op, first, second):
-            nc.vector.scalar_tensor_tensor(values, first, 0.0, second[:], ALU.max, op)
+        def first_bank(g):
+            return first_product(G * g, "bank_first")
 
-        def quantised(values, name):
-            width = values.shape[1] // 4
-            codes = ring.tile([P, width], U32, name=name + "_codes", align_bytes=64)
-            plane = ring.tile([P, width], U8, name=name + "_plane", align_bytes=64)
-            nc.vector.quantize_mx(out=codes[:].bitcast(FP8X4), scales=plane[:], in_=values)
-            return codes, plane
+        def second_values(g):
+            return rectified(first_product(V + G * g, "bank_second"), "second")
 
-        def second_product(g, low, high, last=False):
-            acc = psum.tile([P, G], F32, name="bank_second") if last else psum_out.tile([P, G], F32, name="acc")
-            for b, (codes, plane) in enumerate((low, high)):
-                nc.tensor.matmul_mx(out=acc[:], lhsT=band_words[b][:].bitcast(FP8X4),
-                                    lhsT_scale=band_scales[:, N * b:N * (b + 1)],
-                                    rhs=codes.bitcast(FP8X4), rhs_scale=plane, start=(b == 0), stop=(b == 1))
-            nc.scalar.activation(result[:, G * g:G * (g + 1)], acc[:], ACT.Copy, scale=0.5)
-
-        identity = keep.tile([P, P], F32, name="identity")
-        make_identity(nc, identity[:])
-
-        def turned_product(entry, name):
+        def turned_values(entry, name):
             bank = psum.tile([P, H], F32, name="bank_second")
             words = picked[entry // SLICE][:, entry % SLICE:entry % SLICE + G]
             nc.tensor.matmul_mx(out=bank[:], lhsT=words.bitcast(FP8X4), lhsT_scale=x_plane[:, entry:entry + G],
@@ -143,55 +141,97 @@ def tile_picked_haar_relu_p_kernel(tc, x_words, x_scales, w1, w2_words, w2_scale
                                      start=(k == 0), stop=(k == 1), is_transpose=True)
             nc.scalar.copy(values, bank[:].rearrange("p t v -> p v t"))
 
+        def band_tile(name, groups):
+            return keep.tile([P, 2, groups * G, 4], BF16, name=name, align_bytes=64)
+
+        def vector_band(values, op, bank, second):
+            nc.vector.scalar_tensor_tensor(values, bank, 0.0, second[:], ALU.max, op)
+
+        def quantised(values, name):
+            width = values.shape[1] // 4
+            codes = keep.tile([P, width], U32, name=name + "_codes", align_bytes=64)
+            plane = keep.tile([P, width], U8, name=name + "_plane", align_bytes=64)
+            nc.vector.quantize_mx(out=codes[:].bitcast(FP8X4), scales=plane[:], in_=values)
+            return codes, plane
+
+        result = keep.tile([P, V], F32, name="result")
+
+        def second_product(g, low, high, pool=psum_out, tag="acc"):
+            width = low[1].shape[1]
+            acc = pool.tile([P, width], F32, name=tag)
+            for b, (codes, plane) in enumerate((low, high)):
+                nc.tensor.matmul_mx(out=acc[:], lhsT=band_words[b][:].bitcast(FP8X4),
+                                    lhsT_scale=band_scales[:, N * b:N * (b + 1)],
+                                    rhs=codes.bitcast(FP8X4), rhs_scale=plane, start=(b == 0), stop=(b == 1))
+            nc.scalar.activation(result[:, G * g:G * g + width], acc[:], ACT.Copy, scale=0.5)
+
+        def finish(g, bands):
+            width = bands.shape[2]
+            codes, plane = quantised(bands[:].rearrange("p b v t -> p (b v t)"), "bands%d" % g)
+            second_product(g, (codes[:, :width], plane[:, :width]), (codes[:, width:], plane[:, width:]))
+
         def store(a, b):
             nc.sync.dma_start(out[:, G * a:G * b], result[:, G * a:G * b])
 
-        def both_bands(g, both):
-            codes, plane = quantised(both[:].rearrange("p b v t -> p (b v t)"), "both")
-            return g, (codes[:, :G], plane[:, :G]), (codes[:, G:], plane[:, G:])
+        warm_bank = psum_out.tile([P, SLICE], F32, name="acc")
+        for repeat in range(3):
+            nc.tensor.matmul_mx(out=warm_bank[:], lhsT=picked[2][:, :P].bitcast(FP8X4), lhsT_scale=picked_scales[:, :P],
+                                rhs=picked[2][:].bitcast(FP8X4), rhs_scale=picked_scales[:, :SLICE], start=True, stop=True)
+        low, high = 0, 1
+        bands = {g: band_tile("bands%d" % g, 1) for g in range(V // G)}
+        second, bank = {}, {}
 
-        second = {3: rectified(first_product(V + G * 3, "bank_second"), "second")}
-        turned_second = turned_product(V + G * 2, "turned_second")
-        bank = {3: first_product(G * 3, "bank_first")}
-        second[4] = rectified(first_product(V + G * 4, "bank_second"), "second")
-        turned_first = turned_product(G * 2, "turned_first")
+        def vector_low(g):
+            vector_band(bands[g][:, low], ALU.add, bank[g], second[g])
+
+        def vector_high(g):
+            vector_band(bands[g][:, high], ALU.subtract, bank[g], second[g])
+
+        def shared_high(g):
+            values = keep.tile([P, G, 4], BF16, name="high%d" % g, align_bytes=64)
+            nc.gpsimd.tensor_tensor(values[:], rectified(bank[g], "first")[:], second[g][:], ALU.subtract)
+            return values
+
+        def flat(values):
+            return values.rearrange("p v t -> p (v t)")
+
+        def finish_apart(g, low_values, high_values, pool=psum_out, tag="acc"):
+            low_codes, low_plane = quantised(flat(low_values), "low%d" % g)
+            high_codes, high_plane = quantised(flat(high_values), "high%d" % g)
+            second_product(g, (low_codes[:], low_plane[:]), (high_codes[:], high_plane[:]), pool, tag)
+
+        second[3] = second_values(3)
+        bank[3] = first_bank(3)
+        turned_second = turned_values(V + G * 2, "turned_second")
         turned_negative = keep.tile([P, H], F32, name="turned_negative")
         nc.gpsimd.tensor_scalar(turned_negative[:], turned_second[:], -1.0, 0.0, ALU.mult, ALU.add)
-        second[5] = rectified(first_product(V + G * 5, "bank_second"), "second")
-        extra = ring.tile([P, 2, G, 4], BF16, name="both", align_bytes=64)
-        band(extra[:, 0, :, :], ALU.add, bank[3], second[3])
-        band(extra[:, 1, :, :], ALU.subtract, bank[3], second[3])
-        extra_group = 3
-        for shared, alone in ((4, 5), (0, 1)):
-            if shared not in second:
-                second[shared] = rectified(first_product(V + G * shared, "bank_second"), "second")
-            bank[shared] = first_product(G * shared, "bank_first")
-            shared_first = rectified(bank[shared], "first")
-            if alone not in second:
-                second[alone] = rectified(first_product(V + G * alone, "bank_second"), "second")
-            bank[alone] = first_product(G * alone, "bank_first")
-            if shared == 0:
-                extra = ring.tile([P, 2, G, 4], BF16, name="both", align_bytes=64)
-                turned_sum(extra[:, 0, :, :], turned_first, turned_second)
-                turned_sum(extra[:, 1, :, :], turned_first, turned_negative)
-                extra_group = 2
-            shared_high = keep.tile([P, G, 4], BF16, name="shared_high", align_bytes=64)
-            alone_high = ring.tile([P, G, 4], BF16, name="alone_high", align_bytes=64)
-            lows = ring.tile([P, 2, G, 4], BF16, name="lows", align_bytes=64)
-            nc.gpsimd.tensor_tensor(shared_high[:], shared_first[:], second[shared][:], ALU.subtract)
-            band(alone_high[:], ALU.subtract, bank[alone], second[alone])
-            band(lows[:, 0, :, :], ALU.add, bank[alone], second[alone])
-            band(lows[:, 1, :, :], ALU.add, bank[shared], second[shared])
-            if shared != 0:
-                second_product(*both_bands(extra_group, extra))
-            alone_codes, alone_plane = quantised(alone_high[:].rearrange("p v t -> p (v t)"), "alone_high")
-            low_codes, low_plane = quantised(lows[:].rearrange("p g v t -> p (g v t)"), "lows")
-            shared_codes, shared_plane = quantised(shared_high[:].rearrange("p v t -> p (v t)"), "shared_high")
-            second_product(alone, (low_codes[:, :G], low_plane[:, :G]), (alone_codes[:], alone_plane[:]))
-            second_product(shared, (low_codes[:, G:], low_plane[:, G:]), (shared_codes[:], shared_plane[:]))
-            if shared == 0:
-                store(0, 2)
-                second_product(*both_bands(extra_group, extra), last=True)
-                store(2, 3)
-            else:
-                store(3, 6)
+        second[4] = second_values(4)
+        turned_first = turned_values(G * 2, "turned_first")
+        bank[4] = first_bank(4)
+        vector_low(3)
+        vector_high(3)
+        second[5] = second_values(5)
+        bank[5] = first_bank(5)
+        second[1] = second_values(1)
+        bank[1] = first_bank(1)
+        high1 = shared_high(1)
+        vector_low(4)
+        second[0] = second_values(0)
+        turned_sum(bands[2][:, low], turned_first, turned_second)
+        bank[0] = first_bank(0)
+        turned_sum(bands[2][:, high], turned_first, turned_negative)
+        finish(3, bands[3])
+        vector_high(4)
+        vector_low(5)
+        finish(4, bands[4])
+        vector_high(5)
+        vector_low(1)
+        vector_low(0)
+        finish(5, bands[5])
+        store(3, 6)
+        vector_high(0)
+        finish_apart(1, bands[1][:, low], high1[:], psum, "bank_second")
+        finish(2, bands[2])
+        store(1, 3)
+        finish_apart(0, bands[0][:, low], bands[0][:, high], psum, "bank_second")
+        store(0, 1)

@@ -178,7 +178,7 @@ def tile_picked_haar_relu_p_kernel(tc, x_words, x_scales, w1, w2_words, w2_scale
             nc.tensor.matmul_mx(out=warm_bank[:], lhsT=picked[2][:, :P].bitcast(FP8X4), lhsT_scale=picked_scales[:, :P],
                                 rhs=picked[2][:].bitcast(FP8X4), rhs_scale=picked_scales[:, :SLICE], start=True, stop=True)
         low, high = 0, 1
-        bands = {g: band_tile("bands%d" % g, 1) for g in range(V // G)}
+        bands = {g: band_tile("bands%d" % g, 1) for g in range(V // G - 1)}
         second, bank = {}, {}
 
         def vector_low(g):
@@ -206,32 +206,34 @@ def tile_picked_haar_relu_p_kernel(tc, x_words, x_scales, w1, w2_words, w2_scale
         turned_negative = keep.tile([P, H], F32, name="turned_negative")
         nc.gpsimd.tensor_scalar(turned_negative[:], turned_second[:], -1.0, 0.0, ALU.mult, ALU.add)
         second[4] = second_values(4)
-        turned_first = turned_values(G * 2, "turned_first")
+        second[5] = second_values(5)
         bank[4] = first_bank(4)
+        first5 = rectified(first_bank(5), "first")
         vector_low(3)
         vector_high(3)
-        second[5] = second_values(5)
-        bank[5] = first_bank(5)
         second[1] = second_values(1)
         bank[1] = first_bank(1)
-        high1 = shared_high(1)
+        turned_first = turned_values(G * 2, "turned_first")
         vector_low(4)
-        second[0] = second_values(0)
-        turned_sum(bands[2][:, low], turned_first, turned_second)
-        bank[0] = first_bank(0)
-        turned_sum(bands[2][:, high], turned_first, turned_negative)
-        finish(3, bands[3])
         vector_high(4)
-        vector_low(5)
+        second[0] = second_values(0)
+        bank[0] = first_bank(0)
+        finish(3, bands[3])
         finish(4, bands[4])
-        vector_high(5)
+        store(3, 5)
+        turned_sum(bands[2][:, low], turned_first, turned_second)
+        turned_sum(bands[2][:, high], turned_first, turned_negative)
+        bands[5] = keep.tile([P, 2, G, 4], BF16, name="bands5", tag="bands4", align_bytes=64)
+        nc.gpsimd.tensor_tensor(bands[5][:, low], first5[:], second[5][:], ALU.add)
+        nc.gpsimd.tensor_tensor(bands[5][:, high], first5[:], second[5][:], ALU.subtract)
         vector_low(1)
+        vector_high(1)
         vector_low(0)
-        finish(5, bands[5])
-        store(3, 6)
         vector_high(0)
-        finish_apart(1, bands[1][:, low], high1[:], psum, "bank_second")
-        finish(2, bands[2])
-        store(1, 3)
-        finish_apart(0, bands[0][:, low], bands[0][:, high], psum, "bank_second")
-        store(0, 1)
+        finish(1, bands[1])
+        finish(0, bands[0])
+        store(0, 2)
+        finish_apart(5, bands[5][:, low], bands[5][:, high], psum, "bank_first")
+        store(5, 6)
+        finish_apart(2, bands[2][:, low], bands[2][:, high], psum, "bank_first")
+        store(2, 3)

@@ -165,10 +165,10 @@ def tile_picked_haar_relu_p_kernel(tc, x_words, x_scales, w1, w2_words, w2_scale
                                     rhs=codes.bitcast(FP8X4), rhs_scale=plane, start=(b == 0), stop=(b == 1))
             nc.scalar.activation(result[:, G * g:G * g + width], acc[:], ACT.Copy, scale=0.5)
 
-        def finish(g, bands):
+        def finish(g, bands, pool=psum_out, tag="acc"):
             width = bands.shape[2]
             codes, plane = quantised(bands[:].rearrange("p b v t -> p (b v t)"), "bands%d" % g)
-            second_product(g, (codes[:, :width], plane[:, :width]), (codes[:, width:], plane[:, width:]))
+            second_product(g, (codes[:, :width], plane[:, :width]), (codes[:, width:], plane[:, width:]), pool, tag)
 
         def store(a, b):
             nc.sync.dma_start(out[:, G * a:G * b], result[:, G * a:G * b])
@@ -200,6 +200,14 @@ def tile_picked_haar_relu_p_kernel(tc, x_words, x_scales, w1, w2_words, w2_scale
             high_codes, high_plane = quantised(flat(high_values), "high%d" % g)
             second_product(g, (low_codes[:], low_plane[:]), (high_codes[:], high_plane[:]), pool, tag)
 
+
+        def late_finish(g, k, pool, tag):
+            codes = keep.tile([P, 2 * G], U32, name="late_codes%d" % g, align_bytes=64)
+            plane = reused.tile([P, 2 * G], U8, name="late_plane%d" % g, align_bytes=64, offset=LAST + 2 * G * k)
+            nc.vector.quantize_mx(out=codes[:].bitcast(FP8X4), scales=plane[:], in_=bands[g][:].rearrange("p b v t -> p (b v t)"))
+            second_product(g, (codes[:, :G], plane[:, :G]), (codes[:, G:], plane[:, G:]), pool, tag)
+
+        LAST = T + 16 * H
         second[3] = second_values(3)
         bank[3] = first_bank(3)
         turned_second = turned_values(V + G * 2, "turned_second")
@@ -208,7 +216,8 @@ def tile_picked_haar_relu_p_kernel(tc, x_words, x_scales, w1, w2_words, w2_scale
         second[4] = second_values(4)
         second[5] = second_values(5)
         bank[4] = first_bank(4)
-        first5 = rectified(first_bank(5), "first")
+        bank[5] = first_bank(5)
+        first5 = rectified(bank[5], "first")
         vector_low(3)
         vector_high(3)
         second[1] = second_values(1)
@@ -216,7 +225,8 @@ def tile_picked_haar_relu_p_kernel(tc, x_words, x_scales, w1, w2_words, w2_scale
         turned_first = turned_values(G * 2, "turned_first")
         vector_low(4)
         vector_high(4)
-        second[0] = second_values(0)
+        second[0] = reused.tile([P, G, 4], F32, name="second0", align_bytes=64, offset=LAST)
+        nc.scalar.activation(second[0][:], first_product(V, "bank_second"), ACT.Relu)
         bank[0] = first_bank(0)
         finish(3, bands[3])
         finish(4, bands[4])
@@ -224,16 +234,18 @@ def tile_picked_haar_relu_p_kernel(tc, x_words, x_scales, w1, w2_words, w2_scale
         turned_sum(bands[2][:, low], turned_first, turned_second)
         turned_sum(bands[2][:, high], turned_first, turned_negative)
         bands[5] = keep.tile([P, 2, G, 4], BF16, name="bands5", tag="bands4", align_bytes=64)
-        nc.gpsimd.tensor_tensor(bands[5][:, low], first5[:], second[5][:], ALU.add)
+        cut = 3 * G // 4
         nc.gpsimd.tensor_tensor(bands[5][:, high], first5[:], second[5][:], ALU.subtract)
+        nc.gpsimd.tensor_tensor(bands[5][:, low, :cut], first5[:, :cut], second[5][:, :cut], ALU.add)
         vector_low(1)
         vector_high(1)
+        vector_band(bands[5][:, low, cut:], ALU.add, bank[5][:, cut:], second[5][:, cut:])
         vector_low(0)
         vector_high(0)
-        finish(1, bands[1])
-        finish(0, bands[0])
+        late_finish(1, 0, psum_out, "acc")
+        finish(0, bands[0], psum, "bank_first")
         store(0, 2)
-        finish_apart(5, bands[5][:, low], bands[5][:, high], psum, "bank_first")
+        late_finish(5, 1, psum, "bank_first")
         store(5, 6)
         finish_apart(2, bands[2][:, low], bands[2][:, high], psum, "bank_first")
         store(2, 3)

@@ -34,8 +34,10 @@ def tile_picked_haar_relu_p_kernel(tc, x_words, x_scales, w1, w2_words, w2_scale
 
         scale_table = reused.tile([P, T], U8, name="scale_table", align_bytes=64, offset=0)
         nc.gpsimd.memset(scale_table[:].bitcast(I32)[:TABLE_ROW, :], 0)
-        x_plane = keep.tile([P, S], U8, name="x_plane", align_bytes=64)
-        nc.vector.memset(x_plane[:].bitcast(I32), 0)
+        late_plane = keep.tile([P, 2 * SLICE], U8, name="late_plane", align_bytes=64)
+        early_plane = keep.tile([P, SLICE], U8, name="early_plane", align_bytes=64)
+        for plane in (early_plane, late_plane):
+            nc.vector.memset(plane[:].bitcast(I32), 0)
         identity = keep.tile([P, P], F32, name="identity")
         make_identity(nc, identity[:])
 
@@ -43,7 +45,6 @@ def tile_picked_haar_relu_p_kernel(tc, x_words, x_scales, w1, w2_words, w2_scale
         nc.sync.dma_start(offsets[:], offs)
         nc.sync.dma_start(scale_table[:].bitcast(I32)[TABLE_ROW:, :], x_scales[0].bitcast(I32))
         w1_rows = w1.rearrange("(p j) c -> p j c", j=4)
-        w1_raw = [keep.tile([P, 4, HALF], F32, name="w1_raw%d" % u) for u in range(2)]
         x_table = keep.tile([P, T], U32, name="x_table", align_bytes=64)
         x_rows = x_words[0].rearrange("p n r -> p (n r)").bitcast(I32)
 
@@ -52,13 +53,24 @@ def tile_picked_haar_relu_p_kernel(tc, x_words, x_scales, w1, w2_words, w2_scale
             return tile
 
         nc.sync.dma_start(x_table[:].bitcast(I32), x_rows)
-        for u in range(2):
-            nc.sync.dma_start(w1_raw[u][:], w1_rows[:, :, u * HALF:(u + 1) * HALF])
 
-        picked_scales = keep.tile([P, S], U8, name="picked_scales", align_bytes=64)
-        nc.vector.tensor_copy(picked_scales[:], scale_table[:].indirect(offsets[:]))
-        for r in range(4):
-            nc.sync.dma_start(x_plane[:].bitcast(I32)[r:P:32, :], picked_scales[:].bitcast(I32)[TABLE_ROW + r:P:4, :])
+        def move_scale_rows(plane, rows):
+            for r in range(4):
+                nc.sync.dma_start(plane[:].bitcast(I32)[r:P:32, :], rows[:].bitcast(I32)[TABLE_ROW + r:P:4, :])
+
+        RAW = T + 20 * H
+        early_scales = reused.tile([P, SLICE], U8, name="early_scales", align_bytes=64, offset=RAW + 32 * HALF - SLICE // 2)
+        nc.vector.tensor_copy(early_scales[:], scale_table[:].indirect(offsets[:, 2 * SLICE // 16:]))
+        early_rows = keep.tile([P, SLICE], U8, name="early_rows", align_bytes=64)
+        nc.vector.tensor_copy(early_rows[:].bitcast(I32), early_scales[:].bitcast(I32))
+        move_scale_rows(early_plane, early_rows)
+        w1_both = reused.tile([P, 8 * HALF], F32, name="w1_both", align_bytes=64, offset=RAW)
+        w1_raw = [w1_both[:, 4 * HALF * u:4 * HALF * (u + 1)].rearrange("p (j c) -> p j c", j=4) for u in range(2)]
+        for u in range(2):
+            nc.sync.dma_start(w1_raw[u], w1_rows[:, :, u * HALF:(u + 1) * HALF])
+        late_scales = reused.tile([P, 2 * SLICE], U8, name="late_scales", align_bytes=64, offset=RAW + 32 * HALF)
+        nc.vector.tensor_copy(late_scales[:], scale_table[:].indirect(offsets[:, :2 * SLICE // 16]))
+        move_scale_rows(late_plane, late_scales)
 
         band_words = [load_band_words(words, reused.tile([P, N], U32, name="band_words%d" % b, align_bytes=64, offset=4 * N * b))
                       for b, words in enumerate((w2_words, w3_words))]
@@ -84,7 +96,7 @@ def tile_picked_haar_relu_p_kernel(tc, x_words, x_scales, w1, w2_words, w2_scale
         def cast_half(u, cut):
             values = reused.tile([P, 4, M, 4], BF16, name="w1_bf%d" % u, align_bytes=64, offset=T + 4 * H * u)
             dealt = values[:].rearrange("p t m j -> p m j t")
-            source = w1_raw[u][:].rearrange("p j (m t) -> p m j t", t=4)
+            source = w1_raw[u].rearrange("p j (m t) -> p m j t", t=4)
             nc.scalar.activation(dealt[:, :cut], source[:, :cut], ACT.Copy)
             if cut < M:
                 nc.vector.tensor_copy(dealt[:, cut:], source[:, cut:])
@@ -103,13 +115,18 @@ def tile_picked_haar_relu_p_kernel(tc, x_words, x_scales, w1, w2_words, w2_scale
             quantise_half(u, halves[u])
         gather_words(1, T + 4 * H)
 
+        def picked_plane(entry, count):
+            if entry >= 2 * SLICE:
+                return early_plane[:, entry - 2 * SLICE:entry - 2 * SLICE + count]
+            return late_plane[:, entry:entry + count]
+
         def first_product(entry, tag):
             bank = psum.tile([P, 4, G], F32, name=tag)
             words = picked[entry // SLICE][:, entry % SLICE:entry % SLICE + G]
             for t in range(4):
                 nc.tensor.matmul_mx(out=bank[:, t, :], lhsT=w1_codes[:, P * t:P * (t + 1)].bitcast(FP8X4),
                                     lhsT_scale=w1_plane[:, P * t:P * (t + 1)],
-                                    rhs=words.bitcast(FP8X4), rhs_scale=x_plane[:, entry:entry + G],
+                                    rhs=words.bitcast(FP8X4), rhs_scale=picked_plane(entry, G),
                                     start=True, stop=True)
             return bank[:].rearrange("p t v -> p v t")
 
@@ -127,7 +144,7 @@ def tile_picked_haar_relu_p_kernel(tc, x_words, x_scales, w1, w2_words, w2_scale
         def turned_values(entry, name):
             bank = psum.tile([P, H], F32, name="bank_second")
             words = picked[entry // SLICE][:, entry % SLICE:entry % SLICE + G]
-            nc.tensor.matmul_mx(out=bank[:], lhsT=words.bitcast(FP8X4), lhsT_scale=x_plane[:, entry:entry + G],
+            nc.tensor.matmul_mx(out=bank[:], lhsT=words.bitcast(FP8X4), lhsT_scale=picked_plane(entry, G),
                                 rhs=w1_codes[:].bitcast(FP8X4), rhs_scale=w1_plane[:], start=True, stop=True)
             values = keep.tile([P, H], F32, name=name)
             nc.scalar.activation(values[:], bank[:], ACT.Relu)
@@ -175,8 +192,8 @@ def tile_picked_haar_relu_p_kernel(tc, x_words, x_scales, w1, w2_words, w2_scale
 
         warm_bank = psum_out.tile([P, SLICE], F32, name="acc")
         for repeat in range(3):
-            nc.tensor.matmul_mx(out=warm_bank[:], lhsT=picked[2][:, :P].bitcast(FP8X4), lhsT_scale=picked_scales[:, :P],
-                                rhs=picked[2][:].bitcast(FP8X4), rhs_scale=picked_scales[:, :SLICE], start=True, stop=True)
+            nc.tensor.matmul_mx(out=warm_bank[:], lhsT=picked[2][:, :P].bitcast(FP8X4), lhsT_scale=early_plane[:, :P],
+                                rhs=picked[2][:].bitcast(FP8X4), rhs_scale=early_plane[:], start=True, stop=True)
         low, high = 0, 1
         bands = {g: band_tile("bands%d" % g, 1) for g in range(V // G - 1)}
         second, bank = {}, {}

@@ -99,7 +99,7 @@ def tile_picked_haar_relu_p_kernel(tc, x_words, x_scales, w1, w2_words, w2_scale
             source = w1_raw[u].rearrange("p j (m t) -> p m j t", t=4)
             nc.scalar.activation(dealt[:, :cut], source[:, :cut], ACT.Copy)
             if cut < M:
-                nc.vector.tensor_copy(dealt[:, cut:], source[:, cut:])
+                nc.vector.tensor_copy(values[:].rearrange("p t m j -> p m t j")[:, cut:], w1_raw[u].rearrange("p j (m t) -> p m t j", t=4)[:, cut:])
             return values
 
         def quantise_half(u, values):

@@ -21,6 +21,7 @@ G = 128
 SLICE = 512
 TABLE_ROW = P - 16
 HALF = H // 2
+PIECE = H // 4
 
 
 def tile_picked_haar_relu_p_kernel(tc, x_words, x_scales, w1, w2_words, w2_scales, w3_words, w3_scales, offs, out):
@@ -65,9 +66,9 @@ def tile_picked_haar_relu_p_kernel(tc, x_words, x_scales, w1, w2_words, w2_scale
         nc.vector.tensor_copy(early_rows[:].bitcast(I32), early_scales[:].bitcast(I32))
         move_scale_rows(early_plane, early_rows)
         w1_both = reused.tile([P, 8 * HALF], F32, name="w1_both", align_bytes=64, offset=RAW)
-        w1_raw = [w1_both[:, 4 * HALF * u:4 * HALF * (u + 1)].rearrange("p (j c) -> p j c", j=4) for u in range(2)]
-        for u in range(2):
-            nc.sync.dma_start(w1_raw[u], w1_rows[:, :, u * HALF:(u + 1) * HALF])
+        w1_raw = [w1_both[:, 4 * PIECE * u:4 * PIECE * (u + 1)].rearrange("p (j c) -> p j c", j=4) for u in range(4)]
+        for u in range(4):
+            nc.sync.dma_start(w1_raw[u], w1_rows[:, :, u * PIECE:(u + 1) * PIECE])
         late_scales = reused.tile([P, 2 * SLICE], U8, name="late_scales", align_bytes=64, offset=RAW + 32 * HALF)
         nc.vector.tensor_copy(late_scales[:], scale_table[:].indirect(offsets[:, :2 * SLICE // 16]))
         move_scale_rows(late_plane, late_scales)
@@ -95,11 +96,13 @@ def tile_picked_haar_relu_p_kernel(tc, x_words, x_scales, w1, w2_words, w2_scale
 
         def cast_half(u, cut):
             values = reused.tile([P, 4, M, 4], BF16, name="w1_bf%d" % u, align_bytes=64, offset=T + 4 * H * u)
-            dealt = values[:].rearrange("p t m j -> p m j t")
-            source = w1_raw[u].rearrange("p j (m t) -> p m j t", t=4)
-            nc.scalar.activation(dealt[:, :cut], source[:, :cut], ACT.Copy)
-            if cut < M:
-                nc.vector.tensor_copy(values[:].rearrange("p t m j -> p m t j")[:, cut:], w1_raw[u].rearrange("p j (m t) -> p m t j", t=4)[:, cut:])
+            for k in range(2):
+                part = values[:, :, k * M // 2:(k + 1) * M // 2, :]
+                raw = w1_raw[2 * u + k]
+                end = cut if k == 1 else M // 2
+                nc.scalar.activation(part.rearrange("p t m j -> p m j t")[:, :end], raw.rearrange("p j (m t) -> p m j t", t=4)[:, :end], ACT.Copy)
+                if end < M // 2:
+                    nc.vector.tensor_copy(part.rearrange("p t m j -> p m t j")[:, end:], raw.rearrange("p j (m t) -> p m t j", t=4)[:, end:])
             return values
 
         def quantise_half(u, values):
@@ -110,7 +113,7 @@ def tile_picked_haar_relu_p_kernel(tc, x_words, x_scales, w1, w2_words, w2_scale
 
         gather_words(2, T + 8 * H)
         gather_words(0, T + 12 * H)
-        halves = [cast_half(0, M), cast_half(1, M // 2)]
+        halves = [cast_half(0, M // 2), cast_half(1, M // 4)]
         for u in range(2):
             quantise_half(u, halves[u])
         gather_words(1, T + 4 * H)

@@ -30,8 +30,7 @@ def tile_picked_haar_relu_p_kernel(tc, x_words, x_scales, w1, w2_words, w2_scale
         keep = ctx.enter_context(tc.tile_pool(name="keep", bufs=1))
         reused = ctx.enter_context(tc.tile_pool(name="reused", bufs=1))
         ring = ctx.enter_context(tc.tile_pool(name="ring", bufs=3))
-        psum = ctx.enter_context(tc.psum_pool(name="psum", bufs=3))
-        psum_out = ctx.enter_context(tc.psum_pool(name="psum_out", bufs=2))
+        psum = ctx.enter_context(tc.psum_pool(name="psum", bufs=1))
 
         scale_table = reused.tile([P, T], U8, name="scale_table", align_bytes=64, offset=0)
         nc.gpsimd.memset(scale_table[:].bitcast(I32)[:TABLE_ROW, :], 0)
@@ -138,14 +137,14 @@ def tile_picked_haar_relu_p_kernel(tc, x_words, x_scales, w1, w2_words, w2_scale
             nc.scalar.activation(values[:], bank, ACT.Relu)
             return values
 
-        def first_bank(g):
-            return first_product(G * g, "bank_first")
+        def first_bank(g, tag):
+            return first_product(G * g, tag)
 
-        def second_values(g):
-            return rectified(first_product(V + G * g, "bank_second"), "second")
+        def second_values(g, tag):
+            return rectified(first_product(V + G * g, tag), "second")
 
-        def turned_values(entry, name):
-            bank = psum.tile([P, H], F32, name="bank_second")
+        def turned_values(entry, name, tag):
+            bank = psum.tile([P, H], F32, name=tag)
             words = picked[entry // SLICE][:, entry % SLICE:entry % SLICE + G]
             nc.tensor.matmul_mx(out=bank[:], lhsT=words.bitcast(FP8X4), lhsT_scale=picked_plane(entry, G),
                                 rhs=w1_codes[:].bitcast(FP8X4), rhs_scale=w1_plane[:], start=True, stop=True)
@@ -153,13 +152,10 @@ def tile_picked_haar_relu_p_kernel(tc, x_words, x_scales, w1, w2_words, w2_scale
             nc.scalar.activation(values[:], bank[:], ACT.Relu)
             return values
 
-        def turned_sum(values, first, second):
-            bank = psum.tile([P, 4, G], F32, name="bank_second")
+        def turn_into(bank, part, opens):
             for t in range(4):
-                for k, part in enumerate((first, second)):
-                    nc.tensor.matmul(bank[:, t, :], part[:, P * t:P * (t + 1)], identity[:],
-                                     start=(k == 0), stop=(k == 1), is_transpose=True)
-            nc.scalar.copy(values, bank[:].rearrange("p t v -> p v t"))
+                nc.tensor.matmul(bank[:, t, :], part[:, P * t:P * (t + 1)], identity[:],
+                                 start=(opens and t == 0), stop=(not opens and t == 3), is_transpose=True)
 
         def band_tile(name, groups):
             return keep.tile([P, 2, groups * G, 4], BF16, name=name, align_bytes=64)
@@ -176,7 +172,7 @@ def tile_picked_haar_relu_p_kernel(tc, x_words, x_scales, w1, w2_words, w2_scale
 
         result = keep.tile([P, V], F32, name="result")
 
-        def second_product(g, low, high, pool=psum_out, tag="acc"):
+        def second_product(g, low, high, pool, tag):
             width = low[1].shape[1]
             acc = pool.tile([P, width], F32, name=tag)
             for b, (codes, plane) in enumerate((low, high)):
@@ -185,7 +181,7 @@ def tile_picked_haar_relu_p_kernel(tc, x_words, x_scales, w1, w2_words, w2_scale
                                     rhs=codes.bitcast(FP8X4), rhs_scale=plane, start=(b == 0), stop=(b == 1))
             nc.scalar.activation(result[:, G * g:G * g + width], acc[:], ACT.Copy, scale=0.5)
 
-        def finish(g, bands, pool=psum_out, tag="acc"):
+        def finish(g, bands, pool, tag):
             width = bands.shape[2]
             codes, plane = quantised(bands[:].rearrange("p b v t -> p (b v t)"), "bands%d" % g)
             second_product(g, (codes[:, :width], plane[:, :width]), (codes[:, width:], plane[:, width:]), pool, tag)
@@ -193,7 +189,7 @@ def tile_picked_haar_relu_p_kernel(tc, x_words, x_scales, w1, w2_words, w2_scale
         def store(a, b):
             nc.sync.dma_start(out[:, G * a:G * b], result[:, G * a:G * b])
 
-        warm_bank = psum_out.tile([P, SLICE], F32, name="acc")
+        warm_bank = psum.tile([P, SLICE], F32, name="bank7")
         for repeat in range(3):
             nc.tensor.matmul_mx(out=warm_bank[:], lhsT=picked[2][:, :P].bitcast(FP8X4), lhsT_scale=early_plane[:, :P],
                                 rhs=picked[2][:].bitcast(FP8X4), rhs_scale=early_plane[:], start=True, stop=True)
@@ -215,7 +211,7 @@ def tile_picked_haar_relu_p_kernel(tc, x_words, x_scales, w1, w2_words, w2_scale
         def flat(values):
             return values.rearrange("p v t -> p (v t)")
 
-        def finish_apart(g, low_values, high_values, pool=psum_out, tag="acc"):
+        def finish_apart(g, low_values, high_values, pool, tag):
             low_codes, low_plane = quantised(flat(low_values), "low%d" % g)
             high_codes, high_plane = quantised(flat(high_values), "high%d" % g)
             second_product(g, (low_codes[:], low_plane[:]), (high_codes[:], high_plane[:]), pool, tag)
@@ -228,31 +224,36 @@ def tile_picked_haar_relu_p_kernel(tc, x_words, x_scales, w1, w2_words, w2_scale
             second_product(g, (codes[:, :G], plane[:, :G]), (codes[:, G:], plane[:, G:]), pool, tag)
 
         LAST = T + 16 * H
-        second[3] = second_values(3)
-        bank[3] = first_bank(3)
-        turned_second = turned_values(V + G * 2, "turned_second")
+        second[3] = second_values(3, "bank0")
+        bank[3] = first_bank(3, "bank2")
+        turned_second = turned_values(V + G * 2, "turned_second", "bank1")
         turned_negative = keep.tile([P, H], F32, name="turned_negative")
         nc.gpsimd.tensor_scalar(turned_negative[:], turned_second[:], -1.0, 0.0, ALU.mult, ALU.add)
-        second[4] = second_values(4)
-        second[5] = second_values(5)
-        bank[4] = first_bank(4)
-        bank[5] = first_bank(5)
+        second[4] = second_values(4, "bank3")
+        second[5] = second_values(5, "bank0")
+        bank[4] = first_bank(4, "bank4")
+        bank[5] = first_bank(5, "bank1")
         first5 = rectified(bank[5], "first")
         vector_low(3)
         vector_high(3)
-        second[1] = second_values(1)
-        bank[1] = first_bank(1)
-        turned_first = turned_values(G * 2, "turned_first")
+        second[1] = second_values(1, "bank3")
+        bank[1] = first_bank(1, "bank2")
+        turned_first = turned_values(G * 2, "turned_first", "bank0")
         vector_low(4)
         vector_high(4)
         second[0] = reused.tile([P, G, 4], F32, name="second0", align_bytes=64, offset=LAST)
-        nc.scalar.activation(second[0][:], first_product(V, "bank_second"), ACT.Relu)
-        bank[0] = first_bank(0)
-        finish(3, bands[3])
-        finish(4, bands[4])
+        nc.scalar.activation(second[0][:], first_product(V, "bank4"), ACT.Relu)
+        bank[0] = first_bank(0, "bank5")
+        sums = [psum.tile([P, 4, G], F32, name="bank%d" % (6 + b)) for b in (low, high)]
+        turn_into(sums[low], turned_second, True)
+        turn_into(sums[high], turned_negative, True)
+        finish(3, bands[3], psum, "bank3")
+        for b in (low, high):
+            turn_into(sums[b], turned_first, False)
+        finish(4, bands[4], psum, "bank0")
         store(3, 5)
-        turned_sum(bands[2][:, low], turned_first, turned_second)
-        turned_sum(bands[2][:, high], turned_first, turned_negative)
+        for b in (low, high):
+            nc.scalar.copy(bands[2][:, b], sums[b][:].rearrange("p t v -> p v t"))
         bands[5] = keep.tile([P, 2, G, 4], BF16, name="bands5", tag="bands4", align_bytes=64)
         cut = 3 * G // 4
         nc.gpsimd.tensor_tensor(bands[5][:, high], first5[:], second[5][:], ALU.subtract)
@@ -262,10 +263,10 @@ def tile_picked_haar_relu_p_kernel(tc, x_words, x_scales, w1, w2_words, w2_scale
         vector_band(bands[5][:, low, cut:], ALU.add, bank[5][:, cut:], second[5][:, cut:])
         vector_low(0)
         vector_high(0)
-        late_finish(1, 0, psum_out, "acc")
-        finish(0, bands[0], psum, "bank_first")
+        late_finish(1, 0, psum, "bank4")
+        finish(0, bands[0], psum, "bank2")
         store(0, 2)
-        late_finish(5, 1, psum, "bank_first")
+        late_finish(5, 1, psum, "bank1")
         store(5, 6)
-        finish_apart(2, bands[2][:, low], bands[2][:, high], psum, "bank_first")
+        finish_apart(2, bands[2][:, low], bands[2][:, high], psum, "bank3")
         store(2, 3)

@@ -243,11 +243,11 @@ def tile_picked_haar_relu_p_kernel(tc, x_words, x_scales, w1, w2_words, w2_scale
         vector_high(4)
         second[0] = reused.tile([P, G, 4], F32, name="second0", align_bytes=64, offset=LAST)
         nc.scalar.activation(second[0][:], first_product(V, "bank4"), ACT.Relu)
-        bank[0] = first_bank(0, "bank5")
+        bank[0] = first_bank(0, "bank3")
         sums = [psum.tile([P, 4, G], F32, name="bank%d" % (6 + b)) for b in (low, high)]
         turn_into(sums[low], turned_second, True)
         turn_into(sums[high], turned_negative, True)
-        finish(3, bands[3], psum, "bank3")
+        finish(3, bands[3], psum, "bank5")
         for b in (low, high):
             turn_into(sums[b], turned_first, False)
         finish(4, bands[4], psum, "bank0")
@@ -268,5 +268,5 @@ def tile_picked_haar_relu_p_kernel(tc, x_words, x_scales, w1, w2_words, w2_scale
         store(0, 2)
         late_finish(5, 1, psum, "bank1")
         store(5, 6)
-        finish_apart(2, bands[2][:, low], bands[2][:, high], psum, "bank3")
+        finish_apart(2, bands[2][:, low], bands[2][:, high], psum, "bank5")
         store(2, 3)

from contextlib import ExitStack

import concourse.mybir as mybir
from concourse.masks import make_identity

K, T, S, V, H, N = 512, 4096, 1536, 768, 512, 128
FLOPS = 2 * K * H * S + 2 * 2 * H * N * V

F32 = mybir.dt.float32
BF16 = mybir.dt.bfloat16
I32 = mybir.dt.int32
U32 = mybir.dt.uint32
U16 = mybir.dt.uint16
U8 = mybir.dt.uint8
FP8X4 = mybir.dt.float8_e4m3fn_x4
ALU = mybir.AluOpType
ACT = mybir.ActivationFunctionType

P = 128
G = 128
SLICE = 512
TABLE_ROW = P - 16
HALF = H // 2
PIECE = H // 4


def tile_picked_haar_relu_p_kernel(tc, x_words, x_scales, w1, w2_words, w2_scales, w3_words, w3_scales, offs, out):
    nc = tc.nc
    with ExitStack() as ctx:
        keep = ctx.enter_context(tc.tile_pool(name="keep", bufs=1))
        reused = ctx.enter_context(tc.tile_pool(name="reused", bufs=1))
        ring = ctx.enter_context(tc.tile_pool(name="ring", bufs=3))
        psum = ctx.enter_context(tc.psum_pool(name="psum", bufs=1))

        scale_table = reused.tile([P, T], U8, name="scale_table", align_bytes=64, offset=0)
        nc.gpsimd.memset(scale_table[:].bitcast(I32)[:TABLE_ROW, :], 0)
        late_plane = keep.tile([P, 2 * SLICE], U8, name="late_plane", align_bytes=64)
        early_plane = keep.tile([P, SLICE], U8, name="early_plane", align_bytes=64)
        for plane in (early_plane, late_plane):
            nc.vector.memset(plane[:].bitcast(I32), 0)
        identity = keep.tile([P, P], F32, name="identity")
        make_identity(nc, identity[:])

        offsets = keep.tile([P, S // 16], U16, name="offsets")
        nc.sync.dma_start(offsets[:], offs)
        nc.sync.dma_start(scale_table[:].bitcast(I32)[TABLE_ROW:, :], x_scales[0].bitcast(I32))
        w1_rows = w1.rearrange("(p j) c -> p j c", j=4)
        x_table = keep.tile([P, T], U32, name="x_table", align_bytes=64)
        x_rows = x_words[0].rearrange("p n r -> p (n r)").bitcast(I32)

        def load_band_words(words, tile):
            nc.sync.dma_start(tile[:].bitcast(I32), words[0].rearrange("p n r -> p (n r)").bitcast(I32))
            return tile

        nc.sync.dma_start(x_table[:].bitcast(I32), x_rows)

        def move_scale_rows(plane, rows):
            for r in range(4):
                nc.sync.dma_start(plane[:].bitcast(I32)[r:P:32, :], rows[:].bitcast(I32)[TABLE_ROW + r:P:4, :])

        RAW = T + 20 * H
        early_scales = reused.tile([P, SLICE], U8, name="early_scales", align_bytes=64, offset=RAW + 32 * HALF - SLICE // 2)
        nc.vector.tensor_copy(early_scales[:], scale_table[:].indirect(offsets[:, 2 * SLICE // 16:]))
        early_rows = keep.tile([P, SLICE], U8, name="early_rows", align_bytes=64)
        nc.vector.tensor_copy(early_rows[:].bitcast(I32), early_scales[:].bitcast(I32))
        move_scale_rows(early_plane, early_rows)
        w1_both = reused.tile([P, 8 * HALF], F32, name="w1_both", align_bytes=64, offset=RAW)
        w1_raw = [w1_both[:, 4 * PIECE * u:4 * PIECE * (u + 1)].rearrange("p (j c) -> p j c", j=4) for u in range(4)]
        for u in range(4):
            nc.sync.dma_start(w1_raw[u], w1_rows[:, :, u * PIECE:(u + 1) * PIECE])
        late_scales = reused.tile([P, 2 * SLICE], U8, name="late_scales", align_bytes=64, offset=RAW + 32 * HALF)
        nc.vector.tensor_copy(late_scales[:], scale_table[:].indirect(offsets[:, :2 * SLICE // 16]))
        move_scale_rows(late_plane, late_scales)

        band_words = [load_band_words(words, reused.tile([P, N], U32, name="band_words%d" % b, align_bytes=64, offset=4 * N * b))
                      for b, words in enumerate((w2_words, w3_words))]
        band_scales = reused.tile([P, 2 * N], U8, name="band_scales", align_bytes=64, offset=8 * N)
        nc.gpsimd.memset(band_scales[:].bitcast(I32), 0)
        for b, scales in enumerate((w2_scales, w3_scales)):
            for q in range(4):
                nc.sync.dma_start(
                    band_scales[:].bitcast(I32)[32 * q:32 * q + 4, b * (N // 4):(b + 1) * (N // 4)],
                    scales[0, 4 * q:4 * q + 4, :].bitcast(I32))

        w1_codes = keep.tile([P, H], U32, name="w1_codes", align_bytes=64)
        w1_plane = keep.tile([P, H], U8, name="w1_plane", align_bytes=64)
        M = HALF // 4
        picked = {}

        def gather_words(s, offset):
            words = reused.tile([P, SLICE], U32, name="picked%d" % s, align_bytes=64, offset=offset)
            cols = slice(s * (SLICE // 16), (s + 1) * (SLICE // 16))
            nc.vector.tensor_copy(words[:], x_table[:].indirect(offsets[:, cols]))
            picked[s] = words

        def cast_half(u, cut):
            values = reused.tile([P, 4, M, 4], BF16, name="w1_bf%d" % u, align_bytes=64, offset=T + 4 * H * u)
            for k in range(2):
                part = values[:, :, k * M // 2:(k + 1) * M // 2, :]
                raw = w1_raw[2 * u + k]
                end = cut if k == 1 else M // 2
                nc.scalar.activation(part.rearrange("p t m j -> p m j t")[:, :end], raw.rearrange("p j (m t) -> p m j t", t=4)[:, :end], ACT.Copy)
                if end < M // 2:
                    nc.vector.tensor_copy(part.rearrange("p t m j -> p m t j")[:, end:], raw.rearrange("p j (m t) -> p m t j", t=4)[:, end:])
            return values

        def quantise_half(u, values):
            for t in range(4):
                cols = slice(P * t + M * u, P * t + M * (u + 1))
                nc.vector.quantize_mx(out=w1_codes[:, cols].bitcast(FP8X4), scales=w1_plane[:, cols],
                                      in_=values[:, t, :, :].rearrange("p m j -> p (m j)"))

        gather_words(2, T + 8 * H)
        gather_words(0, T + 12 * H)
        halves = [cast_half(0, M // 2), cast_half(1, M // 4)]
        for u in range(2):
            quantise_half(u, halves[u])
        gather_words(1, T + 4 * H)

        def picked_plane(entry, count):
            if entry >= 2 * SLICE:
                return early_plane[:, entry - 2 * SLICE:entry - 2 * SLICE + count]
            return late_plane[:, entry:entry + count]

        def first_product(entry, tag):
            bank = psum.tile([P, 4, G], F32, name=tag)
            words = picked[entry // SLICE][:, entry % SLICE:entry % SLICE + G]
            for t in range(4):
                nc.tensor.matmul_mx(out=bank[:, t, :], lhsT=w1_codes[:, P * t:P * (t + 1)].bitcast(FP8X4),
                                    lhsT_scale=w1_plane[:, P * t:P * (t + 1)],
                                    rhs=words.bitcast(FP8X4), rhs_scale=picked_plane(entry, G),
                                    start=True, stop=True)
            return bank[:].rearrange("p t v -> p v t")

        def rectified(bank, name):
            values = ring.tile([P, G, 4], F32, name=name, bufs=6)
            nc.scalar.activation(values[:], bank, ACT.Relu)
            return values

        def first_bank(g, tag):
            return first_product(G * g, tag)

        def second_values(g, tag):
            return rectified(first_product(V + G * g, tag), "second")

        def turned_values(entry, name, tag):
            bank = psum.tile([P, H], F32, name=tag)
            words = picked[entry // SLICE][:, entry % SLICE:entry % SLICE + G]
            nc.tensor.matmul_mx(out=bank[:], lhsT=words.bitcast(FP8X4), lhsT_scale=picked_plane(entry, G),
                                rhs=w1_codes[:].bitcast(FP8X4), rhs_scale=w1_plane[:], start=True, stop=True)
            values = keep.tile([P, H], F32, name=name)
            nc.scalar.activation(values[:], bank[:], ACT.Relu)
            return values

        def turn_into(bank, part, opens):
            for t in range(4):
                nc.tensor.matmul(bank[:, t, :], part[:, P * t:P * (t + 1)], identity[:],
                                 start=(opens and t == 0), stop=(not opens and t == 3), is_transpose=True)

        def band_tile(name, groups):
            return keep.tile([P, 2, groups * G, 4], BF16, name=name, align_bytes=64)

        def vector_band(values, op, bank, second):
            nc.vector.scalar_tensor_tensor(values, bank, 0.0, second[:], ALU.max, op)

        def quantised(values, name):
            width = values.shape[1] // 4
            codes = keep.tile([P, width], U32, name=name + "_codes", align_bytes=64)
            plane = keep.tile([P, width], U8, name=name + "_plane", align_bytes=64)
            nc.vector.quantize_mx(out=codes[:].bitcast(FP8X4), scales=plane[:], in_=values)
            return codes, plane

        result = keep.tile([P, V], F32, name="result")

        def second_product(g, low, high, pool, tag):
            width = low[1].shape[1]
            acc = pool.tile([P, width], F32, name=tag)
            for b, (codes, plane) in enumerate((low, high)):
                nc.tensor.matmul_mx(out=acc[:], lhsT=band_words[b][:].bitcast(FP8X4),
                                    lhsT_scale=band_scales[:, N * b:N * (b + 1)],
                                    rhs=codes.bitcast(FP8X4), rhs_scale=plane, start=(b == 0), stop=(b == 1))
            nc.scalar.activation(result[:, G * g:G * g + width], acc[:], ACT.Copy, scale=0.5)

        def finish(g, bands, pool, tag):
            width = bands.shape[2]
            codes, plane = quantised(bands[:].rearrange("p b v t -> p (b v t)"), "bands%d" % g)
            second_product(g, (codes[:, :width], plane[:, :width]), (codes[:, width:], plane[:, width:]), pool, tag)

        def store(a, b):
            nc.sync.dma_start(out[:, G * a:G * b], result[:, G * a:G * b])

        warm_bank = psum.tile([P, SLICE], F32, name="bank7")
        for repeat in range(3):
            nc.tensor.matmul_mx(out=warm_bank[:], lhsT=picked[2][:, :P].bitcast(FP8X4), lhsT_scale=early_plane[:, :P],
                                rhs=picked[2][:].bitcast(FP8X4), rhs_scale=early_plane[:], start=True, stop=True)
        low, high = 0, 1
        bands = {g: band_tile("bands%d" % g, 1) for g in range(V // G - 1)}
        second, bank = {}, {}

        def vector_low(g):
            vector_band(bands[g][:, low], ALU.add, bank[g], second[g])

        def vector_high(g):
            vector_band(bands[g][:, high], ALU.subtract, bank[g], second[g])

        def shared_high(g):
            values = keep.tile([P, G, 4], BF16, name="high%d" % g, align_bytes=64)
            nc.gpsimd.tensor_tensor(values[:], rectified(bank[g], "first")[:], second[g][:], ALU.subtract)
            return values

        def flat(values):
            return values.rearrange("p v t -> p (v t)")

        def finish_apart(g, low_values, high_values, pool, tag):
            low_codes, low_plane = quantised(flat(low_values), "low%d" % g)
            high_codes, high_plane = quantised(flat(high_values), "high%d" % g)
            second_product(g, (low_codes[:], low_plane[:]), (high_codes[:], high_plane[:]), pool, tag)


        def late_finish(g, k, pool, tag):
            codes = keep.tile([P, 2 * G], U32, name="late_codes%d" % g, align_bytes=64)
            plane = reused.tile([P, 2 * G], U8, name="late_plane%d" % g, align_bytes=64, offset=LAST + 2 * G * k)
            nc.vector.quantize_mx(out=codes[:].bitcast(FP8X4), scales=plane[:], in_=bands[g][:].rearrange("p b v t -> p (b v t)"))
            second_product(g, (codes[:, :G], plane[:, :G]), (codes[:, G:], plane[:, G:]), pool, tag)

        LAST = T + 16 * H
        second[3] = second_values(3, "bank0")
        bank[3] = first_bank(3, "bank2")
        turned_second = turned_values(V + G * 2, "turned_second", "bank1")
        turned_negative = keep.tile([P, H], F32, name="turned_negative")
        nc.gpsimd.tensor_scalar(turned_negative[:], turned_second[:], -1.0, 0.0, ALU.mult, ALU.add)
        second[4] = second_values(4, "bank3")
        second[5] = second_values(5, "bank0")
        bank[4] = first_bank(4, "bank4")
        bank[5] = first_bank(5, "bank1")
        first5 = rectified(bank[5], "first")
        vector_low(3)
        vector_high(3)
        second[1] = second_values(1, "bank3")
        bank[1] = first_bank(1, "bank2")
        turned_first = turned_values(G * 2, "turned_first", "bank0")
        vector_low(4)
        vector_high(4)
        second[0] = reused.tile([P, G, 4], F32, name="second0", align_bytes=64, offset=LAST)
        nc.scalar.activation(second[0][:], first_product(V, "bank4"), ACT.Relu)
        bank[0] = first_bank(0, "bank3")
        sums = [psum.tile([P, 4, G], F32, name="bank%d" % (6 + b)) for b in (low, high)]
        turn_into(sums[low], turned_second, True)
        turn_into(sums[high], turned_negative, True)
        finish(3, bands[3], psum, "bank5")
        for b in (low, high):
            turn_into(sums[b], turned_first, False)
        finish(4, bands[4], psum, "bank0")
        store(3, 5)
        for b in (low, high):
            nc.scalar.copy(bands[2][:, b], sums[b][:].rearrange("p t v -> p v t"))
        bands[5] = keep.tile([P, 2, G, 4], BF16, name="bands5", tag="bands4", align_bytes=64)
        cut = 3 * G // 4
        nc.gpsimd.tensor_tensor(bands[5][:, high], first5[:], second[5][:], ALU.subtract)
        nc.gpsimd.tensor_tensor(bands[5][:, low, :cut], first5[:, :cut], second[5][:, :cut], ALU.add)
        vector_low(1)
        vector_high(1)
        vector_band(bands[5][:, low, cut:], ALU.add, bank[5][:, cut:], second[5][:, cut:])
        vector_low(0)
        vector_high(0)
        late_finish(1, 0, psum, "bank4")
        finish(0, bands[0], psum, "bank2")
        store(0, 2)
        late_finish(5, 1, psum, "bank1")
        store(5, 6)
        finish_apart(2, bands[2][:, low], bands[2][:, high], psum, "bank5")
        store(2, 3)
